import numpy as np
import ml_dtypes

BF16 = ml_dtypes.bfloat16


def bf(x):
    return np.asarray(x, np.float32).astype(BF16)


def f32(x):
    return np.asarray(x, np.float32)


def f64(x):
    return np.asarray(x).astype(np.float64)


def striped(idx):
    return np.concatenate([l.reshape(-1, 16).T for l in idx])


def rows(idx, k):
    return np.tile(np.repeat(idx, 16, axis=0), (k // (16 * 8), 1))


def look(tab, idx):
    return np.take_along_axis(f64(tab), rows(idx, len(tab)), axis=1)


K, S, V, N, M = 512, 2048, 2048, 2048, 512


def setup_inputs():
    return {"tab": f32(np.random.standard_normal((K, S))), "w": bf(np.random.standard_normal((K, M)) / np.sqrt(K)), "b": f32(0.5 * np.random.standard_normal((M, 1))), "offs": striped(np.random.randint(0, S, (8, N)))}


def reference(tab, w, b, offs):
    idx = np.stack([g.T.reshape(-1) for g in np.split(offs, 8)])
    t = look(tab, idx)
    x = (t >= 0.25) * 0.5
    y = f64(w).T @ x
    return np.maximum(y + f64(b), 0.0)

@@ -1,0 +1,70 @@
+import concourse.mybir as mybir
+
+P = 128
+PIECE = 512
+THRESHOLD, HIGH = 0.25, 0.5
+FLOPS = 2 * 512 * 512 * 2048
+
+F32, BF16, U16 = mybir.dt.float32, mybir.dt.bfloat16, mybir.dt.uint16
+
+
+def tile_lookup_deq_step_relu_kernel(tc, tab, w, b, offs, out):
+    nc = tc.nc
+    rows, columns = tab.shape
+    m_total, n = out.shape
+    row_blocks, m_blocks, pieces = rows // P, m_total // P, n // PIECE
+    list_columns = PIECE // 16
+    relu = mybir.ActivationFunctionType.Relu
+    is_ge, mult = mybir.AluOpType.is_ge, mybir.AluOpType.mult
+
+    with (
+        tc.tile_pool(name="held", bufs=1) as held,
+        tc.tile_pool(name="ring", bufs=4) as ring,
+        tc.psum_pool(name="psum", bufs=1) as psum,
+    ):
+        lists = held.tile([P, n // 16], U16, name="lists")
+        nc.sync.dma_start(lists[:], offs)
+        bias = held.tile([P, m_blocks], F32, name="bias")
+        windows, weights = [], []
+        for r in range(row_blocks):
+            window = held.tile([P, columns], F32, name=f"window{r}")
+            nc.sync.dma_start(window[:], tab[r * P : (r + 1) * P, :])
+            weight = held.tile([P, m_total], BF16, name=f"weight{r}")
+            nc.sync.dma_start(weight[:], w[r * P : (r + 1) * P, :])
+            windows.append(window)
+            weights.append(weight)
+        with nc.allow_non_contiguous_dma(reason="512 biases, one to a partition and block"):
+            nc.scalar.dma_start(bias[:], b.rearrange("(m p) o -> p (m o)", p=P))
+
+        def accumulate(piece, r, banks):
+            offsets = lists[:, piece * list_columns : (piece + 1) * list_columns]
+            step = ring.tile([P, PIECE], F32, name="step")
+            nc.vector.tensor_scalar(step[:], windows[r][:].indirect(offsets), THRESHOLD, HIGH, op0=is_ge, op1=mult)
+            x = ring.tile([P, PIECE], BF16, name="x")
+            nc.gpsimd.tensor_copy(x[:], step[:])
+            for m in range(m_blocks):
+                nc.tensor.matmul(
+                    banks[m][:], weights[r][:, m * P : (m + 1) * P], x[:],
+                    start=(r == 0), stop=(r == row_blocks - 1),
+                )
+
+        def finish(piece, banks):
+            for m in range(m_blocks):
+                result = ring.tile([P, PIECE], F32, name="result")
+                nc.scalar.activation(result[:], banks[m][:], relu, bias=bias[:, m : m + 1])
+                nc.sync.dma_start(out[m * P : (m + 1) * P, piece * PIECE : (piece + 1) * PIECE], result[:])
+
+        def open_banks(piece):
+            return [psum.tile([P, PIECE], F32, name=f"sum{piece}_{m}", tag=f"bank{piece % 2}_{m}") for m in range(m_blocks)]
+
+        first, second = open_banks(0), open_banks(1)
+        for r in range(row_blocks):
+            accumulate(0, r, first)
+            accumulate(1, r, second)
+        finish(0, first)
+        finish(1, second)
+        for piece in range(2, pieces):
+            banks = open_banks(piece)
+            for r in range(row_blocks):
+                accumulate(piece, r, banks)
+            finish(piece, banks)

@@ -40,11 +40,10 @@ def tile_lookup_deq_step_relu_kernel(tc, tab, w, b, offs, out):
             offsets = lists[:, piece * list_columns : (piece + 1) * list_columns]
             step = ring.tile([P, PIECE], F32, name="step")
             nc.vector.tensor_scalar(step[:], windows[r][:].indirect(offsets), THRESHOLD, HIGH, op0=is_ge, op1=mult)
-            x = ring.tile([P, PIECE], BF16, name="x")
-            nc.gpsimd.tensor_copy(x[:], step[:])
+            x = step[:].bitcast(BF16)[:, 1::2]
             for m in range(m_blocks):
                 nc.tensor.matmul(
-                    banks[m][:], weights[r][:, m * P : (m + 1) * P], x[:],
+                    banks[m][:], weights[r][:, m * P : (m + 1) * P], x,
                     start=(r == 0), stop=(r == row_blocks - 1),
                 )
 

@@ -16,6 +16,7 @@ def tile_lookup_deq_step_relu_kernel(tc, tab, w, b, offs, out):
     list_columns = PIECE // 16
     relu = mybir.ActivationFunctionType.Relu
     is_ge, mult = mybir.AluOpType.is_ge, mybir.AluOpType.mult
+    add, maximum = mybir.AluOpType.add, mybir.AluOpType.max
 
     with (
         tc.tile_pool(name="held", bufs=1) as held,
@@ -34,7 +35,7 @@ def tile_lookup_deq_step_relu_kernel(tc, tab, w, b, offs, out):
             windows.append(window)
             weights.append(weight)
         with nc.allow_non_contiguous_dma(reason="512 biases, one to a partition and block"):
-            nc.scalar.dma_start(bias[:], b.rearrange("(m p) o -> p (m o)", p=P))
+            nc.sync.dma_start(bias[:], b.rearrange("(m p) o -> p (m o)", p=P))
 
         def accumulate(piece, r, banks):
             offsets = lists[:, piece * list_columns : (piece + 1) * list_columns]
@@ -50,7 +51,10 @@ def tile_lookup_deq_step_relu_kernel(tc, tab, w, b, offs, out):
         def finish(piece, banks):
             for m in range(m_blocks):
                 result = ring.tile([P, PIECE], F32, name="result")
-                nc.scalar.activation(result[:], banks[m][:], relu, bias=bias[:, m : m + 1])
+                if piece == pieces - 1 and m % 2 == 1:
+                    nc.vector.tensor_scalar(result[:], banks[m][:], bias[:, m : m + 1], 0.0, op0=add, op1=maximum)
+                else:
+                    nc.scalar.activation(result[:], banks[m][:], relu, bias=bias[:, m : m + 1])
                 nc.sync.dma_start(out[m * P : (m + 1) * P, piece * PIECE : (piece + 1) * PIECE], result[:])
 
         def open_banks(piece):

@@ -37,10 +37,13 @@ def tile_lookup_deq_step_relu_kernel(tc, tab, w, b, offs, out):
         with nc.allow_non_contiguous_dma(reason="512 biases, one to a partition and block"):
             nc.sync.dma_start(bias[:], b.rearrange("(m p) o -> p (m o)", p=P))
 
-        def accumulate(piece, r, banks):
+        def look_up(piece, r, tag):
             offsets = lists[:, piece * list_columns : (piece + 1) * list_columns]
-            step = ring.tile([P, PIECE], F32, name="step")
+            step = ring.tile([P, PIECE], F32, name="step", tag=tag)
             nc.vector.tensor_scalar(step[:], windows[r][:].indirect(offsets), THRESHOLD, HIGH, op0=is_ge, op1=mult)
+            return step
+
+        def multiply(step, r, banks):
             x = step[:].bitcast(BF16)[:, 1::2]
             for m in range(m_blocks):
                 nc.tensor.matmul(
@@ -62,12 +65,14 @@ def tile_lookup_deq_step_relu_kernel(tc, tab, w, b, offs, out):
 
         first, second = open_banks(0), open_banks(1)
         for r in range(row_blocks):
-            accumulate(0, r, first)
-            accumulate(1, r, second)
+            multiply(look_up(0, r, "step"), r, first)
+            multiply(look_up(1, r, "step"), r, second)
+            if r == 0:
+                ahead = look_up(2, 0, "ahead")
         finish(0, first)
         finish(1, second)
         for piece in range(2, pieces):
             banks = open_banks(piece)
             for r in range(row_blocks):
-                accumulate(piece, r, banks)
+                multiply(ahead if piece == 2 and r == 0 else look_up(piece, r, "step"), r, banks)
             finish(piece, banks)

import concourse.mybir as mybir

P = 128
PIECE = 512
THRESHOLD, HIGH = 0.25, 0.5
FLOPS = 2 * 512 * 512 * 2048

F32, BF16, U16 = mybir.dt.float32, mybir.dt.bfloat16, mybir.dt.uint16


def tile_lookup_deq_step_relu_kernel(tc, tab, w, b, offs, out):
    nc = tc.nc
    rows, columns = tab.shape
    m_total, n = out.shape
    row_blocks, m_blocks, pieces = rows // P, m_total // P, n // PIECE
    list_columns = PIECE // 16
    relu = mybir.ActivationFunctionType.Relu
    is_ge, mult = mybir.AluOpType.is_ge, mybir.AluOpType.mult
    add, maximum = mybir.AluOpType.add, mybir.AluOpType.max

    with (
        tc.tile_pool(name="held", bufs=1) as held,
        tc.tile_pool(name="ring", bufs=4) as ring,
        tc.psum_pool(name="psum", bufs=1) as psum,
    ):
        lists = held.tile([P, n // 16], U16, name="lists")
        nc.sync.dma_start(lists[:], offs)
        bias = held.tile([P, m_blocks], F32, name="bias")
        windows, weights = [], []
        for r in range(row_blocks):
            window = held.tile([P, columns], F32, name=f"window{r}")
            nc.sync.dma_start(window[:], tab[r * P : (r + 1) * P, :])
            weight = held.tile([P, m_total], BF16, name=f"weight{r}")
            nc.sync.dma_start(weight[:], w[r * P : (r + 1) * P, :])
            windows.append(window)
            weights.append(weight)
        with nc.allow_non_contiguous_dma(reason="512 biases, one to a partition and block"):
            nc.sync.dma_start(bias[:], b.rearrange("(m p) o -> p (m o)", p=P))

        def look_up(piece, r, tag):
            offsets = lists[:, piece * list_columns : (piece + 1) * list_columns]
            step = ring.tile([P, PIECE], F32, name="step", tag=tag)
            nc.vector.tensor_scalar(step[:], windows[r][:].indirect(offsets), THRESHOLD, HIGH, op0=is_ge, op1=mult)
            return step

        def multiply(step, r, banks):
            x = step[:].bitcast(BF16)[:, 1::2]
            for m in range(m_blocks):
                nc.tensor.matmul(
                    banks[m][:], weights[r][:, m * P : (m + 1) * P], x,
                    start=(r == 0), stop=(r == row_blocks - 1),
                )

        def finish(piece, banks):
            for m in range(m_blocks):
                result = ring.tile([P, PIECE], F32, name="result")
                if piece == pieces - 1 and m % 2 == 1:
                    nc.vector.tensor_scalar(result[:], banks[m][:], bias[:, m : m + 1], 0.0, op0=add, op1=maximum)
                else:
                    nc.scalar.activation(result[:], banks[m][:], relu, bias=bias[:, m : m + 1])
                nc.sync.dma_start(out[m * P : (m + 1) * P, piece * PIECE : (piece + 1) * PIECE], result[:])

        def open_banks(piece):
            return [psum.tile([P, PIECE], F32, name=f"sum{piece}_{m}", tag=f"bank{piece % 2}_{m}") for m in range(m_blocks)]

        first, second = open_banks(0), open_banks(1)
        for r in range(row_blocks):
            multiply(look_up(0, r, "step"), r, first)
            multiply(look_up(1, r, "step"), r, second)
            if r == 0:
                ahead = look_up(2, 0, "ahead")
        finish(0, first)
        finish(1, second)
        for piece in range(2, pieces):
            banks = open_banks(piece)
            for r in range(row_blocks):
                multiply(ahead if piece == 2 and r == 0 else look_up(piece, r, "step"), r, banks)
            finish(piece, banks)
